import numpy as np
import ml_dtypes


def mxq(x, axis, fmt="e4m3"):
    dtype, down = {"e4m3": (ml_dtypes.float8_e4m3fn, 7), "e5m2": (ml_dtypes.float8_e5m2, 14)}[fmt]
    v = np.moveaxis(np.asarray(x, np.float32).astype(ml_dtypes.bfloat16).astype(np.float64), axis, -1)
    blocks = v.reshape(v.shape[:-1] + (-1, 32))
    amax = np.abs(blocks).max(-1, keepdims=True)
    byte = np.maximum(np.where(amax > 0, np.frexp(amax)[1] - 1 + 127, 0) - down, 1)
    scale = np.exp2(byte - 127.0)
    codes = (blocks / scale).astype(np.float32).astype(dtype).astype(np.float64)
    return np.moveaxis((codes * scale).reshape(v.shape), -1, axis)


WIDE = False


def mx_kscale(k):
    if not WIDE:
        return np.ones(k)
    levels = np.array([10, -10, 5, -5, 0])
    if k % 512:
        return np.exp2(np.random.permutation(np.resize(levels, k // 32))).repeat(32)
    a = np.empty((k // 512, 16))
    for p in range(k // 512):
        a[p, :8] = np.random.permutation(np.resize(levels, 8))
        for g in range(8):
            far = levels[np.abs(levels - a[p, g]) >= 10]
            a[p, g + 8] = far[np.random.randint(len(far))]
    return np.exp2(a.ravel()).repeat(32)


BF16 = ml_dtypes.bfloat16


def bf(x):
    return np.asarray(x, np.float32).astype(BF16)


def f64(x):
    return np.asarray(x).astype(np.float64)


T, N, M, Q = 1024, 4, 256, 128
D = N * M
R = N * Q


def kron_sum(a, v):
    n, rows_a, cols_a = a.shape
    _, rows_v, cols_v = v.shape
    total = a[0][:, None, :, None] * v[0][None, :, None, :]
    for i in range(1, n):
        total = total + a[i][:, None, :, None] * v[i][None, :, None, :]
    return total.reshape(rows_a * rows_v, cols_a * cols_v)


def erf(z):
    c = np.clip(z, -6.0, 6.0)
    c2 = 2.0 * c * c
    term = c
    total = c
    for n in range(1, 151):
        term = term * c2 / (2 * n + 1)
        total = total + term
    return np.where(np.abs(z) >= 6.0, np.sign(z), 2.0 / np.sqrt(np.pi) * np.exp(-c * c) * total)


def gelu_erf(z):
    return 0.5 * z * (1.0 + erf(z / np.sqrt(2.0)))


def draw0():
    s, t = mx_kscale(D), mx_kscale(R)
    sign = np.where(np.random.standard_normal((N, N, N)) < 0.0, -1.0, 1.0)
    return {
        "x": bf(np.random.standard_normal((T, D)) * s),
        "a": bf(sign * np.random.uniform(0.6, 1.4, (N, N, N)) / np.sqrt(N)),
        "v1": bf(np.random.standard_normal((N, M, Q)) / np.sqrt(D)),
        "v2": bf(1.5 * np.random.standard_normal((N, Q, M)) / np.sqrt(R)),
        "g_down": bf((1.0 + 0.1 * np.random.standard_normal(D)) / s),
        "g_mid": bf((1.0 + 0.1 * np.random.standard_normal(R)) * t),
        "g_up": bf((1.0 + 0.1 * np.random.standard_normal(R)) / t),
    }


def core(x, a, v1, v2, g_down, g_mid, g_up):
    w_down = f64(g_down)[:, None] * kron_sum(f64(a), f64(v1))
    w_up = f64(g_up)[:, None] * kron_sum(f64(a), f64(v2))
    h = mxq(f64(x), 1, "e4m3") @ mxq(w_down, 0, "e4m3")
    u = gelu_erf(h) * f64(g_mid)[None, :]
    return mxq(u, 1, "e4m3") @ mxq(w_up, 0, "e4m3")


def e4m3fn_bytes(y):
    return np.clip(np.asarray(y, np.float64), -448.0, 448.0).astype(np.float32).astype(ml_dtypes.float8_e4m3fn).view(np.uint8)


def e4m3fn_values(b):
    return np.asarray(b, np.uint8).view(ml_dtypes.float8_e4m3fn).astype(np.float64)


def setup_inputs():
    d = draw0()
    x0 = np.asarray(d['x']).astype(np.float64)
    s = (np.max(np.abs(x0), axis=(0,), keepdims=True) / 448.0).astype(np.float32)
    out = {}
    for k, v in d.items():
        if k == 'x':
            out['x_bytes'] = e4m3fn_bytes(x0 / s.astype(np.float64))
            out['x_scale'] = s
        else:
            out[k] = v
    return out


def reference(x_bytes, x_scale, a, v1, v2, g_down, g_mid, g_up):
    return core(e4m3fn_values(x_bytes) * x_scale.astype(np.float64), a, v1, v2, g_down, g_mid, g_up)

from contextlib import ExitStack

import concourse.mybir as mybir
from concourse.masks import make_identity

F32 = mybir.dt.float32
BF16 = mybir.dt.bfloat16
U32 = mybir.dt.uint32
U8 = mybir.dt.uint8
FP8 = mybir.dt.float8_e4m3fn
FP8X4 = mybir.dt.float8_e4m3fn_x4
MULT = mybir.AluOpType.mult
ADD = mybir.AluOpType.add
ACT = mybir.ActivationFunctionType

T, NK, M, Q = 1024, 4, 256, 128
D, R = NK * M, NK * Q
P = 128
FLOPS = 2 * T * D * R * 2
TILES = T // P
PER_LOAD = 4
SUMMED = {3: range(0, 8), 2: range(3, 8)}


def tile_compacterhypercomplexadapter_kernel(tc, x_bytes, x_scale, a, v1, v2, g_down, g_mid, g_up, out):
    nc = tc.nc
    with ExitStack() as ctx:
        keep = ctx.enter_context(tc.tile_pool(name="keep", bufs=1))
        flow = ctx.enter_context(tc.tile_pool(name="flow", bufs=3))
        psum = ctx.enter_context(tc.psum_pool(name="psum", bufs=2))
        ctx.enter_context(tc.manual_schedule())

        a_rows = keep.tile([P, 16], BF16, name="a_rows")
        v1_raw = [keep.tile([P, 512], BF16, name="v1_raw%d" % g) for g in range(2)]
        v2_raw = keep.tile([P, 1024], BF16, name="v2_raw")
        gain_down = [keep.tile([P, 4], BF16, name="gain_down%d" % g) for g in range(2)]
        gain_up = keep.tile([P, 4], BF16, name="gain_up")
        gain_mid = keep.tile([P, 4], BF16, name="gain_mid")
        a_all = keep.tile([P, 64], BF16, name="a_all")
        x_scales = [keep.tile([P, 512], F32, name="x_scales%d" % g) for g in range(2)]
        x_raw = [[keep.tile([P, PER_LOAD, 512], U8, name="x_raw%d_%d" % (h, g)) for g in range(2)] for h in range(TILES // PER_LOAD)]

        v1_view = v1.rearrange("i (g mm t) q -> g mm i (t q)", g=2, t=4)
        gd_view = g_down.rearrange("(r g mm t) -> g r mm t", r=4, g=2, t=4)
        xs_view = x_scale.rearrange("o (r g j) -> g o r j", r=4, g=2)
        x_view = x_bytes.rearrange("(h p a) (r g j) -> h g p a r j", p=P, a=PER_LOAD, r=4, g=2)
        out_view = out.rearrange("(h p a) n -> h a p n", p=P, a=PER_LOAD)

        def load_x(h, g):
            nc.sync.dma_start(out=x_raw[h][g][:].rearrange("p a (r j) -> p a r j", r=4), in_=x_view[h, g])

        def load_scales(g):
            nc.sync.dma_start(out=x_scales[g][:].rearrange("p (r j) -> p r j", r=4), in_=xs_view[g, 0].partition_broadcast(P))

        nc.sync.dma_start(out=v1_raw[0][:], in_=v1_view[0])
        nc.sync.dma_start(out=a_rows[:], in_=a.rearrange("i r c -> i (r c)").partition_broadcast(32))
        nc.sync.dma_start(out=v2_raw[:], in_=v2.rearrange("i (qq t) m -> qq i (t m)", t=4))
        nc.sync.dma_start(out=gain_down[0][:], in_=gd_view[0])
        nc.sync.dma_start(out=v1_raw[1][:], in_=v1_view[1])
        nc.sync.dma_start(out=a_all[:], in_=a.rearrange("i r c -> (i r c)").partition_broadcast(P))
        nc.sync.dma_start(out=gain_down[1][:], in_=gd_view[1])
        nc.sync.dma_start(out=gain_up[:], in_=g_up.rearrange("(p t) -> p t", t=4))
        load_scales(0)
        load_scales(1)
        load_x(0, 0)
        load_x(0, 1)
        nc.sync.dma_start(out=gain_mid[:], in_=g_mid.rearrange("(p t) -> p t", t=4))
        for h in range(1, TILES // PER_LOAD):
            load_x(h, 0)
            load_x(h, 1)

        ident = keep.tile([P, P], F32, name="ident")
        ident_bf = keep.tile([P, P], BF16, name="ident_bf")
        make_identity(nc, ident[:])
        make_identity(nc, ident_bf[:])
        warm = keep.tile([P, 8], F32, name="warm")
        nc.vector.memset(warm[:], 0.0)
        nc.scalar.activation(out=warm[:, 1:2], in_=warm[:, 0:1], func=ACT.Gelu)

        pick = keep.tile([P, 32], F32, name="pick")
        nc.vector.tensor_reduce(out=pick[:], in_=ident[:].rearrange("p (mm i) -> p mm i", i=4), axis=mybir.AxisListType.X, op=ADD)
        mix = keep.tile([P, 4, 4, 32], BF16, name="mix")
        nc.vector.tensor_tensor(
            out=mix[:],
            in0=pick[:].unsqueeze(1).unsqueeze(1).to_broadcast([P, 4, 4, 32]),
            in1=a_rows[:].rearrange("p (r c) -> p c r", c=4).unsqueeze(3).to_broadcast([P, 4, 4, 32]),
            op=MULT,
        )
        v1_mov = [keep.tile([P, 512], BF16, name="v1_mov%d" % g) for g in range(2)]
        for g in range(2):
            nc.scalar.copy(
                out=v1_mov[g][:].rearrange("p (s qq t) -> p s qq t", s=4, t=4),
                in_=v1_raw[g][:].rearrange("p (t qq s) -> p s qq t", t=4, s=4),
            )
        v2_mov = keep.tile([P, 1024], BF16, name="v2_mov")
        nc.vector.tensor_copy(out=v2_mov[:].rearrange("p (m t) -> p m t", t=4), in_=v2_raw[:].rearrange("p (t m) -> p m t", t=4))
        a_f32 = keep.tile([P, 64], F32, name="a_f32")
        nc.vector.tensor_copy(out=a_f32[:], in_=a_all[:])

        def mix_of(c):
            return mix[:, c].rearrange("p r mm -> p (r mm)")

        free_banks = list(range(8))
        held = {}

        def take_bank(key, shape, dtype):
            held[key] = free_banks.pop(0)
            return psum.tile(shape, dtype, name=key[0], tag="bank%d" % held[key], bufs=1)

        def give_bank(key):
            free_banks.append(held[key])

        wd = [keep.tile([P, 4, 4, 128], BF16, name="wd%d" % g, align_bytes=64) for g in range(2)]
        wd_codes = [keep.tile([P, 512], U32, name="wd_codes%d" % g, align_bytes=64) for g in range(2)]
        wd_scales = [keep.tile([P, 512], U8, name="wd_scales%d" % g, align_bytes=64) for g in range(2)]
        banks = {}

        def down_sum(n):
            g, c = divmod(n, 4)
            banks["d", n] = take_bank(("down_sum", n), [P, 512], F32)
            nc.tensor.matmul(out=banks["d", n][:], lhsT=mix_of(c), rhs=v1_mov[g][:], start=True, stop=True)

        def down_gain(n):
            g, c = divmod(n, 4)
            nc.vector.tensor_tensor(
                out=wd[g][:, :, c, :].rearrange("p s (qq t) -> p s qq t", t=4),
                in0=banks["d", n][:].rearrange("p (s qq t) -> p s qq t", s=4, t=4),
                in1=gain_down[g][:].unsqueeze(1).unsqueeze(1).to_broadcast([P, 4, 32, 4]),
                op=MULT,
            )
            give_bank(("down_sum", n))

        def down_quant(g):
            nc.vector.quantize_mx(out=wd_codes[g][:].bitcast(FP8X4), scales=wd_scales[g][:], in_=wd[g][:].rearrange("p s c w -> p (s c w)"))

        wu = [keep.tile([P, 2048], BF16, name="wu%d" % h, align_bytes=64) for h in range(2)]
        wu_codes = [keep.tile([P, 512], U32, name="wu_codes%d" % h, align_bytes=64) for h in range(2)]
        wu_scales = [keep.tile([P, 512], U8, name="wu_scales%d" % h, align_bytes=64) for h in range(2)]
        v2_turned = keep.tile([P, 8, 32, 4], BF16, name="v2_turned")
        terms = {(c, i): keep.tile([P, len(SUMMED[c]), 4, 32], F32, name="terms%d_%d" % (c, i)) for c in SUMMED for i in range(4)}

        def turn_v2():
            banks["v"] = take_bank(("turned",), [P, 1024], BF16)
            for mb in range(8):
                nc.tensor.transpose(banks["v"][:, mb * P:(mb + 1) * P], v2_mov[:, mb * P:(mb + 1) * P], ident_bf[:])

        def turn_v2_out():
            nc.scalar.copy(out=v2_turned[:].rearrange("p mb qq i -> p (mb qq i)"), in_=banks["v"][:])
            give_bank(("turned",))

        def up_terms(c, terms_i=range(4)):
            first = SUMMED[c].start
            for i in terms_i:
                for r in range(4):
                    col = 16 * i + 4 * r + c
                    nc.scalar.activation(out=terms[c, i][:, :, r, :], in_=v2_turned[:, first:8, :, i], func=ACT.Copy, scale=a_f32[:, col:col + 1])

        def up_sum(n):
            c, half = divmod(n, 2)
            acc = take_bank(("up_sum", n), [P, 512], F32)
            banks["u", n] = acc
            summed = [mb for mb in range(4 * half, 4 * half + 4) if mb in SUMMED.get(c, ())]
            width = 512 - P * len(summed)
            if width:
                nc.tensor.matmul(out=acc[:, 0:width], lhsT=mix_of(c), rhs=v2_mov[:, 512 * half:512 * half + width], start=True, stop=True)
            for mb in summed:
                at = P * (mb - 4 * half)
                for i in range(4):
                    nc.tensor.matmul(
                        out=acc[:, at:at + P],
                        lhsT=terms[c, i][:, mb - SUMMED[c].start].rearrange("p r qq -> p (r qq)"),
                        rhs=ident[:],
                        start=(i == 0),
                        stop=(i == 3),
                        is_transpose=True,
                    )

        def up_gain(n):
            nc.vector.tensor_tensor(
                out=wu[n // 4][:, 512 * (n % 4):512 * (n % 4 + 1)].rearrange("p (m t) -> p m t", t=4),
                in0=banks["u", n][:].rearrange("p (m t) -> p m t", t=4),
                in1=gain_up[:].unsqueeze(1).to_broadcast([P, P, 4]),
                op=MULT,
            )
            give_bank(("up_sum", n))

        def up_quant(h):
            nc.vector.quantize_mx(out=wu_codes[h][:].bitcast(FP8X4), scales=wu_scales[h][:], in_=wu[h][:])

        st = {}

        def x_mul(j):
            h, s = divmod(j, PER_LOAD)
            st["xs", j] = flow.tile([P, 1024], BF16, name="x_scaled", tag="x_scaled", bufs=8)
            for g in range(2):
                nc.vector.tensor_tensor(
                    out=st["xs", j][:, 512 * g:512 * (g + 1)],
                    in0=x_raw[h][g][:, s, :].bitcast(FP8),
                    in1=x_scales[g][:],
                    op=MULT,
                )

        def x_turn(j):
            st["xt", j] = take_bank(("x_turned", j), [P, 2, 2, P], F32)
            words = st["xs", j][:].bitcast(F32)
            for g in range(2):
                for u in range(2):
                    nc.tensor.transpose(st["xt", j][:, g, u, :], words[:, 256 * g + u:256 * (g + 1):2], ident[:])

        def x_out(j):
            st["xg", j] = flow.tile([P, 1024], BF16, name="x_grouped", tag="x_grouped", bufs=8, align_bytes=64)
            nc.scalar.copy(
                out=st["xg", j][:].bitcast(F32).rearrange("p (g n u) -> p g n u", g=2, u=2),
                in_=st["xt", j][:].rearrange("p g u n -> p g n u"),
            )
            give_bank(("x_turned", j))

        def x_quant(j):
            st["xc", j] = flow.tile([P, 256], U32, name="x_codes", tag="x_codes", bufs=8, align_bytes=64)
            st["xe", j] = flow.tile([P, 256], U8, name="x_exps", tag="x_exps", bufs=8, align_bytes=64)
            nc.vector.quantize_mx(out=st["xc", j][:].bitcast(FP8X4), scales=st["xe", j][:], in_=st["xg", j][:])

        def down_mm(j):
            st["h", j] = take_bank(("hidden", j), [P, 4, P], F32)
            for s in range(4):
                for g in range(2):
                    nc.tensor.matmul_mx(
                        out=st["h", j][:, s, :],
                        lhsT=wd_codes[g][:, s * P:(s + 1) * P].bitcast(FP8X4),
                        lhsT_scale=wd_scales[g][:, s * P:(s + 1) * P],
                        rhs=st["xc", j][:, g * P:(g + 1) * P].bitcast(FP8X4),
                        rhs_scale=st["xe", j][:, g * P:(g + 1) * P],
                        start=(g == 0),
                        stop=(g == 1),
                    )

        def gelu(j):
            st["ug", j] = flow.tile([P, P, 4], F32, name="gelu", tag="gelu", bufs=8)
            nc.scalar.activation(out=st["ug", j][:], in_=st["h", j][:].rearrange("p s n -> p n s"), func=ACT.Gelu)
            give_bank(("hidden", j))

        def u_mul(j):
            st["ub", j] = flow.tile([P, P, 4], BF16, name="u", tag="u", bufs=8, align_bytes=64)
            nc.vector.tensor_tensor(out=st["ub", j][:], in0=st["ug", j][:], in1=gain_mid[:].unsqueeze(1).to_broadcast([P, P, 4]), op=MULT)

        def u_quant(j):
            st["uc", j] = flow.tile([P, P], U32, name="u_codes", tag="u_codes", bufs=8, align_bytes=64)
            st["ue", j] = flow.tile([P, P], U8, name="u_exps", tag="u_exps", bufs=8, align_bytes=64)
            nc.vector.quantize_mx(out=st["uc", j][:].bitcast(FP8X4), scales=st["ue", j][:], in_=st["ub", j][:].rearrange("p n s -> p (n s)"))

        def up_mm(j, h):
            banks["o", j, h] = take_bank(("result", j, h), [P, 512], F32)
            nc.tensor.matmul_mx(
                out=banks["o", j, h][:],
                lhsT=st["uc", j][:].bitcast(FP8X4),
                lhsT_scale=st["ue", j][:],
                rhs=wu_codes[h][:].bitcast(FP8X4),
                rhs_scale=wu_scales[h][:],
                start=True,
                stop=True,
            )

        def store(j, h, engine="S"):
            rows = flow.tile([P, 512], F32, name="rows", tag="rows", bufs=16)
            if engine == "S":
                nc.scalar.copy(out=rows[:], in_=banks["o", j, h][:])
            else:
                nc.vector.tensor_copy(out=rows[:], in_=banks["o", j, h][:])
            give_bank(("result", j, h))
            nc.sync.dma_start(out=out_view[j // PER_LOAD, j % PER_LOAD][:, 512 * h:512 * (h + 1)], in_=rows[:])

        down_sum(0)
        down_sum(1)
        down_sum(2)
        turn_v2()
        down_sum(3)
        down_sum(4)
        down_sum(5)
        down_sum(6)
        down_gain(0)
        turn_v2_out()
        up_terms(3, [0])
        down_gain(1)
        down_sum(7)
        down_gain(2)
        up_sum(0)
        down_gain(3)
        up_terms(3, [1])
        up_sum(1)
        down_gain(4)
        down_quant(0)
        up_sum(2)
        down_gain(5)
        up_terms(3, [2])
        up_sum(3)
        down_gain(6)
        down_gain(7)
        x_mul(0)
        down_quant(1)
        x_turn(0)
        up_terms(3, [3])
        x_mul(1)
        x_out(0)
        x_turn(1)
        up_gain(0)
        x_quant(0)
        up_terms(2, [0])
        down_mm(0)
        up_gain(1)
        x_out(1)
        x_mul(2)
        up_sum(6)
        gelu(0)
        x_quant(1)
        x_turn(2)
        up_gain(2)
        down_mm(1)
        u_mul(0)
        up_terms(2, [1])
        x_out(2)
        x_mul(3)
        u_quant(0)
        gelu(1)
        x_turn(3)
        x_quant(2)
        up_gain(3)
        down_mm(2)
        up_sum(7)
        u_mul(1)
        up_terms(2, [2])
        x_out(3)
        up_quant(0)
        u_quant(1)
        up_terms(2, [3])
        gelu(2)
        x_mul(4)
        x_quant(3)
        up_mm(0, 0)
        up_sum(4)
        x_turn(4)
        down_mm(3)
        up_sum(5)
        u_mul(2)
        up_gain(6)
        store(0, 0)
        u_quant(2)
        x_out(4)
        gelu(3)
        up_gain(7)
        up_mm(1, 0)
        x_mul(5)
        x_quant(4)
        up_mm(2, 0)
        x_turn(5)
        down_mm(4)
        store(1, 0)
        up_gain(4)
        u_mul(3)
        store(2, 0)
        up_gain(5)
        x_out(5)
        u_quant(3)
        up_quant(1)
        gelu(4)
        up_mm(3, 0)
        x_mul(6)
        up_mm(0, 1)
        up_mm(1, 1)
        x_turn(6)
        store(3, 0)
        x_quant(5)
        u_mul(4)
        down_mm(5)
        store(0, 1)
        x_out(6)
        x_mul(7)
        u_quant(4)
        up_mm(2, 1)
        x_turn(7)
        gelu(5)
        x_quant(6)
        up_mm(3, 1)
        down_mm(6)
        store(1, 1)
        u_mul(5)
        up_mm(4, 0)
        x_out(7)
        store(2, 1)
        u_quant(5)
        x_quant(7)
        up_mm(4, 1)
        gelu(6)
        down_mm(7)
        store(3, 1, "V")
        store(4, 0)
        u_mul(6)
        up_mm(5, 0)
        up_mm(5, 1)
        gelu(7)
        u_quant(6)
        store(4, 1, "V")
        store(5, 0)
        u_mul(7)
        up_mm(6, 0)
        up_mm(6, 1)
        u_quant(7)
        store(5, 1)
        store(6, 0, "V")
        up_mm(7, 0)
        up_mm(7, 1)
        store(6, 1)
        store(7, 0, "V")
        store(7, 1)
